import numpy as np, ml_dtypes
CORES = [50,52,122,124]
N = 4
import mx_ref
NC, ROOT = 384, 2
C = np.float32(0.019)
BF = ml_dtypes.bfloat16
def cut(t, i, w=512):
    return t[:, w * i:w * i + w]
def tile(rs):
    return np.stack(rs, axis=2).reshape(128, -1).astype(BF)
def pick(b):
    s = np.zeros((128, 128, 4), np.float32)
    s[np.arange(128), np.arange(128), b] = 1.0
    return mx_ref.quantize(s.reshape(128, 512).astype(BF))
def pk(c, s, i=0):
    return (np.ascontiguousarray(c[:, 512 * i:512 * i + 512]), mx_ref.live(s[:, 128 * i:128 * i + 128]))
def inputs(rng, e, E):
    def f(*shape):
        v = (rng.standard_normal(shape, dtype=np.float32) * np.exp2(rng.integers(-2, 3, shape[:-1] + (1,)))).astype(BF)
        return mx_ref.spread((v.astype(np.float32) * np.exp2(rng.integers(-E, E + 1, shape[:-2] + (1, 1))).astype(np.float32)).astype(BF), rng, e)
    def packed(k):
        c = np.zeros((N, 128, k * 512), np.uint8); s = np.zeros((N, 128, k * 128), np.uint8)
        for r in range(N):
            for i in range(k):
                a, b = mx_ref.quantize(f(128, 512)); c[r][:, 512 * i:512 * i + 512] = a; s[r][:, 128 * i:128 * i + 128] = mx_ref.plane(b, rng)
        return c, s
    d = {}
    d["wc"], d["ws"] = packed(1)
    d["a"] = f(N, 128, 512)
    d["bb"] = f(N, 128, 4 * 512)
    d["x"] = f(N, 128, 4 * NC)
    return d
def setup_inputs(rng):
    return inputs(rng, 0, 0)
def setup_inputs_blocks(rng):
    return inputs(rng, 2, 0)
def setup_inputs_wide(rng):
    return inputs(rng, 0, 3)
def reference(wc, ws, a, bb, x):
    S = [pick(t) for t in range(4)]; A = mx_ref.quantize(a[ROOT])
    V = [mx_ref.quantize(tile([mx_ref.matmul(S[t], pk(wc[j], ws[j])) + mx_ref.matmul(mx_ref.quantize(cut(bb[j], t)), A) * C for t in range(4)])) for j in range(N)]
    y = np.zeros((N, 128, N * NC), np.float32)
    for r in range(N):
        X = mx_ref.quantize(x[r])
        for j in range(N):
            y[r][:, NC * j:NC * j + NC] = mx_ref.matmul(V[j], X)
    return {"y": y}

from concourse.bass import DstId, RemoteDMATransfer
from concourse.mybir import dt, AluOpType, ActivationFunctionType

N = 4
NC = 384
HALF = NC // 2
C = 0.019

F8 = "float8_e4m3fn_x4"
SCRATCH = {
    "at": ("sbuf", [128, 512], "bfloat16"),
    "bt": ("sbuf", [128, 2048], "bfloat16"),
    "xt": ("sbuf", [128, 4 * NC], "bfloat16"),
    "zt": ("sbuf", [128, 520], "bfloat16"),
    "one": ("sbuf", [128, 128], "bfloat16"),
    "vt": ("sbuf", [128, 512], "bfloat16"),
    "mt": ("sbuf", [128, 512], "float32"),
    "yt": ("sbuf", [128, N * NC], "float32"),
    "wq": ("sbuf", [128, 128], F8), "wp": ("sbuf", [128, 128], "uint8"),
    "ac": ("sbuf", [128, 128], F8), "ap": ("sbuf", [128, 128], "uint8"),
    "sq": ("sbuf", [128, 512], F8), "sp": ("sbuf", [128, 512], "uint8"),
    "bq": ("sbuf", [128, 512], F8), "bp": ("sbuf", [128, 512], "uint8"),
    "xq": ("sbuf", [128, NC], F8), "xp": ("sbuf", [128, NC], "uint8"),
    "ps": ("psum", [128, 512 * 8], "float32"),
}
for _j in range(N):
    SCRATCH["c%d" % _j] = ("sbuf", [128, 128], F8)
    SCRATCH["p%d" % _j] = ("sbuf", [128, 128], "uint8")

SEMAPHORES = ["ld_a", "ld_w", "ld_b", "ld_x", "zz", "sel", "qa", "qs", "qb", "qx", "dd", "rr", "qv", "st", "loc"]
SEMAPHORES += ["m%d" % b for b in range(4)] + ["t%d" % b for b in range(4)]
SEMAPHORES += ["k%d%s" % (i, h) for i in range(N) for h in "uv"] + ["e%d" % i for i in range(N)]
SEMAPHORES += ["in_%s" % t for t in ["ac", "ap"] + ["%s%d" % (k, j) for j in range(N) for k in "cp"]]


def bits(m):
    return [1 << e for e in range(m.bit_length()) if (m >> e) & 1]


def halves(m):
    b = bits(m)
    h = len(b) // 2
    return sum(b[:h]), sum(b[h:])


def plan(T, topo):
    cores = list(T.cores)
    root = cores[T.root]
    near = {c: [d for d in cores if d != c and topo.chip(d) == topo.chip(c)][0] for c in cores}
    far = {c: [d for d in cores if topo.chip(d) != topo.chip(c)] for c in cores}
    porter = {c: all(topo.may_write(c, d) for d in far[c]) for c in cores}
    calls = {c: [] for c in cores}

    def both(c, tile, dests, ready=None):
        for k in "cp":
            name = "a" + k if tile == "a" else "%s%d" % (k, tile)
            calls[c].append((ready or "in_" + name, [(name, d, m) for d, m in dests]))

    def out(c):
        off = topo.mask(c, far[c][0])
        return off, topo.mask(c, near[c]) & ~off

    fport = [d for d in far[root] if porter[d]][0]
    finner = near[fport]
    inner = near[root]
    rk = {c: cores.index(c) for c in cores}
    off, on = out(root)
    lo, hi = halves(off)
    both(root, "a", [(finner, off)], "qa")
    both(root, "a", [(fport, off), (inner, on)], "qa")
    both(root, rk[root], [(finner, lo), (fport, hi), (inner, on)], "qv")
    both(root, rk[inner], [(finner, lo), (fport, hi)])
    both(root, rk[fport], [(inner, on)])
    off, on = out(fport)
    lo, hi = halves(off)
    both(fport, rk[fport], [(root, off), (finner, halves(on)[0])], "qv")
    both(fport, rk[finner], [(root, lo), (inner, hi)])
    for c in (inner, finner):
        off, on = out(c)
        calls[c].append(("qv", [("c%d" % rk[c], near[c], off)]))
        calls[c].append(("qv", [("p%d" % rk[c], near[c], on)]))

    order = {}
    for c in cores:
        w = [d for d in cores if d != c]
        w.sort(key=lambda d: 0 if d == root else 1 if d == near[c] else 2 if porter[d] else 3)
        order[c] = [rk[c]] + [rk[d] for d in w]
    return calls, order


def rank_program(g, core, T, topo):
    rank = T.rank_of(core)
    if rank is None:
        return
    sem = T.sem
    calls, order = plan(T, topo)
    is_root = rank == T.root
    need = {}
    for c in calls:
        for _, ts in calls[c]:
            for name, d, m in ts:
                if d == core:
                    need["in_" + name] = len(bits(m))
    vc, vp = "c%d" % rank, "p%d" % rank
    ps = T.ps

    def bank(k, n):
        return ps[:, 512 * k:512 * k + n]

    if is_root:
        g.sync.dma_start(T.at[:], T.a[:]).then_inc(sem.ld_a, 16)
    g.sync.dma_start(T.bt[:], T.bb[:]).then_inc(sem.ld_b, 16)
    g.scalar.dma_start(T.wq[:].bitcast(dt.uint8), T.wc[:]).then_inc(sem.ld_w, 16)
    g.scalar.dma_start(T.wp[:], T.ws[:]).then_inc(sem.ld_w, 16)
    g.scalar.dma_start(T.xt[:], T.x[:]).then_inc(sem.ld_x, 16)

    g.wait_ge(sem.zz, 2)
    g.affine_select(T.zt[:, 3:515:4], T.one[:], [[-1, 128]], AluOpType.is_equal, 0.0, 0, 1).then_inc(sem.sel, 1)

    g.vector.memset(T.zt[:], 0.0).then_inc(sem.zz, 1)
    g.vector.memset(T.one[:], 1.0).then_inc(sem.zz, 1)
    if is_root:
        g.vector.wait_ge(sem.ld_a, 16)
        g.vector.quantize_mx(T.ac[:], T.ap[:], T.at[:]).then_inc(sem.qa, 1)
    g.vector.wait_ge(sem.zz, 2)
    g.vector.wait_ge(sem.sel, 1)
    for b in range(4):
        s = slice(128 * b, 128 * b + 128)
        g.vector.quantize_mx(T.sq[:, s], T.sp[:, s], T.zt[:, 3 - b:515 - b]).then_inc(sem.qs, 1)
    g.vector.wait_ge(sem.ld_b, 16)
    for b in range(4):
        s = slice(128 * b, 128 * b + 128)
        g.vector.quantize_mx(T.bq[:, s], T.bp[:, s], T.bt[:, 512 * b:512 * b + 512]).then_inc(sem.qb, 1)
    g.vector.wait_ge(sem.ld_x, 16)
    g.vector.quantize_mx(T.xq[:], T.xp[:], T.xt[:]).then_inc(sem.qx, 1)

    te = g.tensor
    te.wait_ge(sem.ld_w, 32)
    te.wait_ge(sem.qs, 4)
    for b in range(4):
        s = slice(128 * b, 128 * b + 128)
        te.matmul_mx(bank(b, 128), T.sq[:, s], T.sp[:, s], T.wq[:], T.wp[:], True, True).then_inc(sem.dd, 1)
    te.wait_ge(sem.qb, 4)
    if is_root:
        te.wait_ge(sem.qa, 1)
    else:
        te.wait_ge(sem.in_ac, need["in_ac"])
        te.wait_ge(sem.in_ap, need["in_ap"])
    for b in range(4):
        s = slice(128 * b, 128 * b + 128)
        te.matmul_mx(bank(4 + b, 128), T.bq[:, s], T.bp[:, s], T.ac[:], T.ap[:], True, True).then_inc(sem["m%d" % b], 1)

    g.vector.wait_ge(sem.dd, 4)
    for b in range(4):
        t = T.mt[:, 128 * b:128 * b + 128]
        g.scalar.wait_ge(sem["m%d" % b], 1)
        g.scalar.activation(t, bank(4 + b, 128), ActivationFunctionType.Copy, scale=C).then_inc(sem["t%d" % b], 1)
        g.vector.wait_ge(sem["t%d" % b], 1)
        g.vector.tensor_tensor(T.vt[:, b:512:4], bank(b, 128), t, AluOpType.add).then_inc(sem.rr, 1)
    g.vector.wait_ge(sem.rr, 4)
    g.vector.quantize_mx(T[vc][:], T[vp][:], T.vt[:]).then_inc(sem.qv, 1)

    sent = 0
    for ready, ts in calls[core]:
        g.wait_ge(sem[ready], need.get(ready, 1))
        trs = []
        for name, d, m in ts:
            v = T[name][:]
            if "c" in name:
                v = v.bitcast(dt.uint8)
            rid, pid, _ = topo.addr(d)
            trs.append((v, name, d, m, rid, pid))
            sent += len(bits(m))
        if len(trs) == 1:
            v, name, d, m, rid, pid = trs[0]
            g.remote_dma(out_ap=v, in_ap=v, remote_sem=sem["in_" + name], local_sem=sem.loc, pid=pid, routing_id=rid, dma_engine_mask=m)
        else:
            g.remote_dma_fused([RemoteDMATransfer(dst_ids=[DstId(rid=rid, pnc=pid)], dma_engine_mask=m, remote_sem=sem["in_" + name], src=v, dst=v)
                                for v, name, d, m, rid, pid in trs], local_sem=sem.loc)
    g.wait_ge(sem.loc, sent)

    te.wait_ge(sem.qx, 1)
    for i, j in enumerate(order[core]):
        if j == rank:
            te.wait_ge(sem.qv, 1)
        else:
            te.wait_ge(sem["in_c%d" % j], need["in_c%d" % j])
            te.wait_ge(sem["in_p%d" % j], need["in_p%d" % j])
        for h, q in enumerate("uv"):
            xs = slice(HALF * h, HALF * h + HALF)
            te.matmul_mx(bank(2 * i + h, HALF), T["c%d" % j][:], T["p%d" % j][:], T.xq[:, xs], T.xp[:, xs], True, True).then_inc(sem["k%d%s" % (i, q)], 1)
        y0 = NC * j
        g.vector.wait_ge(sem["k%du" % i], 1)
        g.vector.tensor_copy(T.yt[:, y0:y0 + HALF], bank(2 * i, HALF)).then_inc(sem["e%d" % i], 1)
        g.scalar.wait_ge(sem["k%dv" % i], 1)
        g.scalar.activation(T.yt[:, y0 + HALF:y0 + NC], bank(2 * i + 1, HALF), ActivationFunctionType.Copy).then_inc(sem["e%d" % i], 1)
        g.sync.wait_ge(sem["e%d" % i], 2)
        g.sync.dma_start(T.y[:, y0:y0 + NC], T.yt[:, y0:y0 + NC]).then_inc(sem.st, 16)
    g.sync.wait_ge(sem.st, 16 * N)
